import numpy as np, ml_dtypes
CORES = [1,2,5,7,57,58,61,63,73,74,77,79]
N = 12
S, B = 2, 128
NT = N * S
def setup_inputs(rng):
    a = (rng.standard_normal((128, 128), dtype=np.float32) / 12).astype(ml_dtypes.bfloat16)
    return {"x": rng.standard_normal((N, 128, S * B), dtype=np.float32).astype(ml_dtypes.bfloat16), "a": np.broadcast_to(a, (N, 128, 128)).copy(), "at": np.broadcast_to(a.T, (N, 128, 128)).copy()}
def setup_inputs_big(rng):
    d = setup_inputs(rng)
    for k in ("x",): d[k] = (d[k].astype(np.float32) * 1048576.0).astype(d[k].dtype)
    return d
def setup_inputs_small(rng):
    d = setup_inputs(rng)
    for k in ("x",): d[k] = (d[k].astype(np.float32) * (1 / 1048576.0)).astype(d[k].dtype)
    return d
def setup_inputs_apart(rng):
    d = setup_inputs(rng)
    f = (10.0 ** rng.permutation(np.linspace(-1.5, 1.5, N))).astype(np.float32).reshape(N, 1, 1)
    for k in ("x",): d[k] = (d[k].astype(np.float32) * f).astype(d[k].dtype)
    return d
def reference(x, a, at):
    A = a[0].astype(np.float64); X = [x[t // S][:, B * (t % S):B * (t % S) + B].astype(np.float64) for t in range(NT)]
    f = [None] * NT; b = [None] * NT; h = np.zeros((128, B))
    for t in range(NT):
        h = A.T @ h + X[t]; f[t] = h
    h = np.zeros((128, B))
    for t in range(NT - 1, -1, -1):
        h = A.T @ h + X[t]; b[t] = h
    return {"y": np.stack([np.concatenate([f[r * S + s] + b[r * S + s] for s in range(S)], axis=1) for r in range(N)]).astype(ml_dtypes.bfloat16)}

from concourse.bass import DstId, RemoteDMATransfer
from concourse.mybir import AluOpType

S, B = 2, 128
W = S * B
GMAX, NG = 4, 3
NPOW = 16

SCRATCH = {
    "xg": ("sbuf", [128, GMAX * W], "bfloat16"),
    "pw": ("sbuf", [128, NPOW * B], "bfloat16"),
    "tp": ("sbuf", [128, 4 * B], "bfloat16"),
    "sm0": ("sbuf", [128, B], "bfloat16"),
    "sm1": ("sbuf", [128, B], "bfloat16"),
    "fr": ("sbuf", [128, NG * B], "bfloat16"),
    "x2": ("sbuf", [128, W], "bfloat16"),
    "ys": ("sbuf", [128, W], "bfloat16"),
    "k0": ("psum", [128, 512], "float32"), "k1": ("psum", [128, 512], "float32"),
    "k2": ("psum", [128, 512], "float32"), "k3": ("psum", [128, 512], "float32"),
    "ps0": ("psum", [128, 512], "float32"), "ps1": ("psum", [128, 512], "float32"),
    "py0": ("psum", [128, 512], "float32"), "py1": ("psum", [128, 512], "float32"),
}
SEMAPHORES = (["ldx", "lda", "ldt", "ls", "st"]
              + ["xa%d" % i for i in range(GMAX)] + ["fa%d" % i for i in range(NG)]
              + ["m_" + n for n in ("a2", "t2", "t4", "a34", "a56", "a78", "t8", "hi", "s0", "s1", "y0", "y1")]
              + ["v_" + n for n in ("a2", "t2", "t4", "a34", "a56", "a78", "t8", "hi", "s0", "s1", "x2", "y")])


def _bits(mask):
    return bin(mask).count("1")


def _plan(cores, topo):
    groups = []
    for c in cores:
        if groups and topo.chip(groups[-1][-1]) == topo.chip(c):
            groups[-1].append(c)
        else:
            groups.append([c])
    flows = []
    for i, gs in enumerate(groups):
        for j, gd in enumerate(groups):
            if i != j:
                cand = [c for c in gs if all(topo.may_write(c, d) for d in gd)]
                flows.append((len(cand), i, j, cand))
    flows.sort()
    load = {c: 0 for c in cores}
    send = {}
    feeder = {}
    for _, i, j, cand in flows:
        d = 0 if i < j else 1
        for dst in groups[j]:
            s = min(cand, key=lambda c: (topo.die(c) != topo.die(dst), load[c], c))
            load[s] += 1
            send.setdefault(s, {}).setdefault(d, []).append(dst)
            feeder[(dst, i)] = s
    return groups, send, feeder, load


def rank_program(g, core, T, topo):
    rank = T.rank_of(core)
    if rank is None:
        return
    groups, send, feeder, load = _plan(T.cores, topo)
    gi = [i for i, gr in enumerate(groups) if core in gr][0]
    grp = groups[gi]
    p = grp.index(core)
    span = [(S * T.rank_of(gr[0]), S * T.rank_of(gr[-1]) + S - 1) for gr in groups]
    first, last = span[gi]
    own = [S * rank + s for s in range(S)]
    sem = T.sem
    pe, ve, sy, sc = g.tensor, g.vector, g.sync, g.scalar
    mine = send.get(core, {})

    def xs(u):
        k = u - first
        return T.xg[:, k * B:(k + 1) * B]

    def pw(k, n=1):
        return T.pw[:, (k - 1) * B:(k - 1 + n) * B]

    def tp(i):
        return T.tp[:, i * B:(i + 1) * B]

    def dst_ids(cs):
        return [DstId(rid=topo.addr(c)[0], pnc=topo.addr(c)[1]) for c in cs]

    def common_mask(cs):
        m = topo.mask(core, cs[0])
        for c in cs[1:]:
            m &= topo.mask(core, c)
        return m

    others = [u for u in range(first, last + 1) if u not in own]
    far = []
    for j in sorted((j for j in range(len(groups)) if j != gi), key=lambda j: (load[feeder[(core, j)]], j)):
        far.append((j, [t - span[j][1] if j < gi else span[j][0] - t for t in own]))
    sums = {d: [(u, last - u if d == 0 else u - first) for u in own + others] for d in mine}
    need = {1}
    need.update(abs(t - u) for t in own for u in others)
    need.update(k for _, ks in far for k in ks)
    need.update(k for d in sums for _, k in sums[d] if k)
    hi = sorted(k for k in need if k > 8)
    need.update(k - 8 for k in hi)
    n56 = 2 if 6 in need else (1 if 5 in need else 0)
    n78 = 2 if 8 in need else (1 if 7 in need else 0)

    seen = set()

    def wait(q, qn, name, val):
        if (qn, name) not in seen:
            seen.add((qn, name))
            q.wait_ge(sem[name], val)

    in_mask = common_mask([c for c in grp if c != core])

    def x_sem(u):
        q = (u - first) // S
        return ("ldx", 16) if q == p else ("xa%d" % q, _bits(in_mask))

    def pow_sem(k):
        if k == 1:
            return ("lda", 16)
        if k > 8:
            return ("v_hi", 1)
        return ("v_" + {2: "a2", 3: "a34", 4: "a34", 5: "a56", 6: "a56", 7: "a78", 8: "a78"}[k], 1)

    def term(out, k, rhs, rhs_sem, start, stop):
        wait(pe, "pe", *pow_sem(k))
        wait(pe, "pe", *rhs_sem)
        return pe.matmul(out, pw(k), rhs, start, stop)

    made = []

    def round_to(name, out, in_):
        ve.wait_ge(sem["m_" + name], 1)
        ve.tensor_copy(out, in_).then_inc(sem["v_" + name], 1)
        made.append("v_" + name)

    myx = T.xg[:, p * W:(p + 1) * W]
    sy.dma_start(myx, T.x[:, :]).then_inc(sem.ldx, 16)
    sc.dma_start(pw(1), T.a[:, :]).then_inc(sem.lda, 16)
    sc.dma_start(tp(0), T.at[:, :]).then_inc(sem.ldt, 16)

    g.wait_ge(sem.ldx, 16)
    peers = [c for c in grp if c != core]
    urgent = [c for c in peers if c in send]
    sent = 0
    for cs in (urgent, [c for c in peers if c not in send]):
        if cs:
            g.remote_dma_fused([RemoteDMATransfer(dst_ids=dst_ids(cs), dma_engine_mask=in_mask, remote_sem=sem["xa%d" % p],
                                                  srcs=[myx], dsts=[myx for _ in cs])], local_sem=sem.ls)
            sent += _bits(in_mask)

    wait(pe, "pe", "lda", 16)
    wait(pe, "pe", "ldt", 16)
    pe.matmul(T.k0[:, 0:B], tp(0), pw(1), True, True).then_inc(sem.m_a2, 1)
    pe.matmul(T.k1[:, 0:B], pw(1), tp(0), True, True).then_inc(sem.m_t2, 1)
    round_to("a2", pw(2), T.k0[:, 0:B])
    round_to("t2", tp(1), T.k1[:, 0:B])
    py = [T.py0[:, 0:B], T.py1[:, 0:B]]
    for s in range(S):
        term(py[s], 1, xs(own[1 - s]), ("ldx", 16), True, False)
    wait(pe, "pe", "v_a2", 1)
    wait(pe, "pe", "v_t2", 1)
    pe.matmul(T.k2[:, 0:B], pw(2), tp(1), True, True).then_inc(sem.m_t4, 1)
    pe.matmul(T.k3[:, 0:2 * B], tp(1), pw(1, 2), True, True).then_inc(sem.m_a34, 1)
    round_to("t4", tp(2), T.k2[:, 0:B])
    round_to("a34", pw(3, 2), T.k3[:, 0:2 * B])
    wait(pe, "pe", "v_t4", 1)
    if n56:
        pe.matmul(T.k0[:, 0:n56 * B], tp(2), pw(1, n56), True, True).then_inc(sem.m_a56, 1)
        round_to("a56", pw(5, n56), T.k0[:, 0:n56 * B])
    wait(pe, "pe", "v_a34", 1)
    if n78:
        pe.matmul(T.k1[:, 0:n78 * B], tp(2), pw(3, n78), True, True).then_inc(sem.m_a78, 1)
        round_to("a78", pw(7, n78), T.k1[:, 0:n78 * B])
    if hi:
        pe.matmul(T.k2[:, 0:B], pw(4), tp(2), True, True).then_inc(sem.m_t8, 1)
        round_to("t8", tp(3), T.k2[:, 0:B])
        lo, nh = hi[0] - 8, hi[-1] - hi[0] + 1
        wait(pe, "pe", "v_t8", 1)
        for k in range(lo, lo + nh):
            wait(pe, "pe", *pow_sem(k))
        pe.matmul(T.k3[:, 0:nh * B], tp(3), pw(lo, nh), True, True).then_inc(sem.m_hi, 1)
        round_to("hi", pw(hi[0], nh), T.k3[:, 0:nh * B])

    for d in sorted(sums):
        ts = [(u, k) for u, k in sums[d] if k]
        for n, (u, k) in enumerate(ts):
            ins = term(T["ps%d" % d][:, 0:B], k, xs(u), x_sem(u), n == 0, n == len(ts) - 1)
        ins.then_inc(sem["m_s%d" % d], 1)
        u0 = [u for u, k in sums[d] if not k][0]
        ve.wait_ge(sem["m_s%d" % d], 1)
        wait(ve, "ve", *x_sem(u0))
        ve.tensor_tensor(T["sm%d" % d][:, :], T["ps%d" % d][:, 0:B], xs(u0), AluOpType.add).then_inc(sem["v_s%d" % d], 1)
        cs = mine[d]
        m = common_mask(cs)
        g.wait_ge(sem["v_s%d" % d], 1)
        land = T.fr[:, gi * B:(gi + 1) * B]
        g.remote_dma_fused([RemoteDMATransfer(dst_ids=dst_ids(cs), dma_engine_mask=m, remote_sem=sem["fa%d" % gi],
                                              srcs=[T["sm%d" % d][:, :]], dsts=[land for _ in cs])], local_sem=sem.ls)
        sent += _bits(m)
    g.wait_ge(sem.ls, sent)

    wait(ve, "ve", "ldx", 16)
    ve.tensor_tensor(T.x2[:, :], myx, myx, AluOpType.add).then_inc(sem.v_x2, 1)
    for u in others:
        for s in range(S):
            term(py[s], abs(own[s] - u), xs(u), x_sem(u), False, False)
    for n, (j, ks) in enumerate(far):
        arr = ("fa%d" % j, _bits(topo.mask(feeder[(core, j)], core)))
        for s in range(S):
            ins = term(py[s], ks[s], T.fr[:, j * B:(j + 1) * B], arr, False, n == len(far) - 1)
            if n == len(far) - 1:
                ins.then_inc(sem["m_y%d" % s], 1)
    for name in made:
        wait(pe, "pe", name, 1)
    ve.wait_ge(sem.v_x2, 1)
    for s in range(S):
        ve.wait_ge(sem["m_y%d" % s], 1)
        ve.tensor_tensor(T.ys[:, s * B:(s + 1) * B], py[s], T.x2[:, s * B:(s + 1) * B], AluOpType.add).then_inc(sem.v_y, 1)
    sy.wait_ge(sem.v_y, S)
    sy.dma_start(T.y[:, :], T.ys[:, :]).then_inc(sem.st, 16)
    sy.wait_ge(sem.st, 16)
